import numpy as np
import ml_dtypes


def mxq(x, axis, fmt="e4m3"):
    dtype, down = {"e4m3": (ml_dtypes.float8_e4m3fn, 7), "e5m2": (ml_dtypes.float8_e5m2, 14)}[fmt]
    v = np.moveaxis(np.asarray(x, np.float32).astype(ml_dtypes.bfloat16).astype(np.float64), axis, -1)
    blocks = v.reshape(v.shape[:-1] + (-1, 32))
    amax = np.abs(blocks).max(-1, keepdims=True)
    byte = np.maximum(np.where(amax > 0, np.frexp(amax)[1] - 1 + 127, 0) - down, 1)
    scale = np.exp2(byte - 127.0)
    codes = (blocks / scale).astype(np.float32).astype(dtype).astype(np.float64)
    return np.moveaxis((codes * scale).reshape(v.shape), -1, axis)


WIDE = False


def mx_kscale(k):
    if not WIDE:
        return np.ones(k)
    levels = np.array([10, -10, 5, -5, 0])
    if k % 512:
        return np.exp2(np.random.permutation(np.resize(levels, k // 32))).repeat(32)
    a = np.empty((k // 512, 16))
    for p in range(k // 512):
        a[p, :8] = np.random.permutation(np.resize(levels, 8))
        for g in range(8):
            far = levels[np.abs(levels - a[p, g]) >= 10]
            a[p, g + 8] = far[np.random.randint(len(far))]
    return np.exp2(a.ravel()).repeat(32)


def f64(x):
    return np.asarray(x).astype(np.float64)


def striped(idx):
    return np.tile(idx.reshape(-1, 16).T, (8, 1)).astype(np.uint16)


def unstriped(offs):
    return offs[:16].T.reshape(-1).astype(np.int64)


E2M1 = np.array([0.0, 0.5, 1.0, 1.5, 2.0, 3.0, 4.0, 6.0, -0.0, -0.5, -1.0, -1.5, -2.0, -3.0, -4.0, -6.0])


def pack_weight(w, fmt):
    k, n = w.shape
    w = f64(np.asarray(w, np.float32).astype(ml_dtypes.bfloat16)).reshape(k // 32, 32, n)
    amax = np.abs(w).max(1)
    if fmt == "e4m3":
        byte = np.frexp(amax)[1] - 1 + 127 - 7
    else:
        mant, ex = np.frexp(amax / 6.0)
        byte = np.where(mant > 0.5, ex, ex - 1) + 127
    byte = np.clip(np.where(amax > 0, byte, 1), 1, 254)
    scaled = (w * np.exp2(127.0 - byte)[:, None, :]).reshape(k, n).astype(np.float32)
    by_word = np.ascontiguousarray(scaled.reshape(k // 512, 128, 4, n).transpose(0, 1, 3, 2))
    if fmt == "e4m3":
        words = by_word.astype(ml_dtypes.float8_e4m3fn).view(np.uint8)
    else:
        c = by_word.astype(ml_dtypes.float4_e2m1fn).view(np.uint8) & 0xF
        words = (c[..., 0::2] | (c[..., 1::2] << 4)).reshape(k // 512, 128, 2 * n)
    return np.ascontiguousarray(words), np.ascontiguousarray(byte.astype(np.uint8).reshape(k // 512, 16, n))


def unpack_weight(words, scales, fmt):
    g, _, n = scales.shape
    words = np.ascontiguousarray(words).reshape(g, 128, n, -1)
    if fmt == "e4m3":
        vals = words.view(ml_dtypes.float8_e4m3fn).astype(np.float64)
    else:
        nib = np.empty((g, 128, n, 4), np.uint8)
        nib[..., 0::2] = words & 0xF
        nib[..., 1::2] = words >> 4
        vals = E2M1[nib]
    vals = vals * np.repeat(np.exp2(scales.astype(np.float64) - 127.0), 8, axis=1)[..., None]
    return vals.transpose(0, 1, 3, 2).reshape(g * 512, n)


def gelu(v):
    return 0.5 * v * (1.0 + np.tanh(np.sqrt(2.0 / np.pi) * (v + 0.044715 * v**3)))


def striped8(idx):
    return np.concatenate([v.reshape(-1, 16).T for v in idx]).astype(np.uint16)


def unstriped8(offs):
    return np.stack([offs[16 * g:16 * g + 16].T.reshape(-1) for g in range(8)]).astype(np.int64)


def runs(v, idx8):
    k = np.arange(v.shape[0])
    return v[k[:, None], idx8[k % 512 // 64]]


T, S, P, K, H, N = 2048, 1024, 512, 1536, 1024, 384

def setup_inputs():
    n = np.random.standard_normal
    s = mx_kscale(K)[:, None]
    u = mx_kscale(H)[:, None]
    d = {}
    d["tab_words"], d["tab_scales"] = pack_weight(n((K, T)) * s, "e4m3")
    d["w1"] = (1.3 * n((K, H)) / K**0.5 / s).astype(np.float32)
    d["b1"] = (0.5 * n(H)).astype(np.float32)
    d["gain"] = (np.exp(0.3 * n(H)) * u[:, 0]).astype(np.float32)
    d["w2_words"], d["w2_scales"] = pack_weight(n((H, H)) / H**0.5 / u * u.T, "e2m1")
    d["w3"] = (n((H, N)) / H**0.5 / u).astype(np.float32)
    d["b3"] = (0.5 * n(N)).astype(np.float32)
    d["offs"] = striped8(np.stack([np.random.permutation(T)[:S] for _ in range(8)]))
    perm = np.random.permutation(S)
    d["pos1"] = striped(perm[:P])
    d["pos2"] = striped(perm[P:])
    return d

def reference(tab_words, tab_scales, w1, b1, gain, w2_words, w2_scales, w3, b3, offs, pos1, pos2):
    v = runs(unpack_weight(tab_words, tab_scales, "e4m3"), unstriped8(offs))
    w2 = unpack_weight(w2_words, w2_scales, "e2m1")
    a = (mxq(f64(w1), 0, "e4m3").T @ v) + f64(b1)[:, None]
    h = f64(gain)[:, None] * (0.5 * a * (1.0 + np.tanh(np.sqrt(2.0 / np.pi) * (a + 0.044715 * a**3))))
    evening = h[:, unstriped(pos1)]
    x = evening - h[:, unstriped(pos2)]
    y = w2.T @ mxq(x, 0, "e4m3")
    z = np.maximum(y, evening)
    return (mxq(f64(w3), 0, "e4m3").T @ mxq(z, 0, "e4m3")) + f64(b3)[:, None]

@@ -1,0 +1,278 @@
+from contextlib import ExitStack
+
+import concourse.mybir as mybir
+
+T, S, PAIRS, K, H, N = 2048, 1024, 512, 1536, 1024, 384
+FLOPS = 2 * (K * H * S + H * H * PAIRS + H * N * PAIRS)
+
+F32 = mybir.dt.float32
+BF16 = mybir.dt.bfloat16
+I32 = mybir.dt.int32
+U32 = mybir.dt.uint32
+U16 = mybir.dt.uint16
+U8 = mybir.dt.uint8
+FP8X4 = mybir.dt.float8_e4m3fn_x4
+FP4X4 = mybir.dt.float4_e2m1fn_x4
+ALU = mybir.AluOpType
+ACT = mybir.ActivationFunctionType
+
+P = 128
+PACK = 4
+KP = P * PACK
+BANK = 512
+K_PASSES = K // KP
+H_PASSES = H // KP
+N_TILES = N // P
+QUARTER = 128
+PLANE_ROW = (0, 8, 4)
+
+
+def tile_list_udder_health_watch_kernel(
+    tc, tab_words, tab_scales, w1, b1, gain, w2_words, w2_scales, w3, b3, offs, pos1, pos2, out
+):
+    nc = tc.nc
+    with ExitStack() as ctx:
+        keep = ctx.enter_context(tc.tile_pool(name="keep", bufs=1))
+        raw = ctx.enter_context(tc.tile_pool(name="raw", bufs=4))
+        rounded = ctx.enter_context(tc.tile_pool(name="rounded", bufs=3))
+        feat = ctx.enter_context(tc.tile_pool(name="feat", bufs=6))
+        psum = ctx.enter_context(tc.psum_pool(name="psum", bufs=8))
+
+        offs_sb = keep.tile([P, S // 16], U16, name="offs_sb")
+        pos1_sb = keep.tile([P, PAIRS // 16], U16, name="pos1_sb")
+        pos2_sb = keep.tile([P, PAIRS // 16], U16, name="pos2_sb")
+        tab_sb = [keep.tile([P, T], I32, name=f"tab{a}") for a in range(K_PASSES)]
+        tab_rows = keep.tile([P, T // 4], I32, name="tab_rows")
+        picked = [keep.tile([P, S], U32, name=f"picked{a}", align_bytes=64) for a in range(K_PASSES)]
+        picked_rows = keep.tile([P, S], U8, name="picked_rows", align_bytes=64)
+        picked_plane = keep.tile([P, S], U8, name="picked_plane", align_bytes=64)
+        b1_sb = keep.tile([P, H_PASSES, PACK], F32, name="b1_sb")
+        gain_sb = keep.tile([P, H_PASSES, PACK], F32, name="gain_sb")
+        b3_sb = keep.tile([P, N_TILES], F32, name="b3_sb")
+        w2_raw = keep.tile([P, H_PASSES, H], U16, name="w2_raw")
+        w2_raw_plane = keep.tile([P, H_PASSES, H], U8, name="w2_raw_plane")
+        w2_codes = keep.tile([P, H_PASSES, H], U16, name="w2_codes", align_bytes=64)
+        w2_plane = keep.tile([P, H_PASSES, H], U8, name="w2_plane", align_bytes=64)
+
+        nc.vector.memset(tab_rows[:], 0)
+        nc.vector.memset(w2_raw_plane[:].rearrange("p a c -> p (a c)").bitcast(I32), 0)
+
+        def load_words(a):
+            nc.sync.dma_start(out=tab_sb[a][:], in_=tab_words[a].rearrange("p t i -> p (t i)").bitcast(I32))
+
+        def load_w1(a, b):
+            t = raw.tile([P, PACK, KP], F32, name="raw")
+            nc.sync.dma_start(
+                out=t[:], in_=w1[a * KP : (a + 1) * KP, b * KP : (b + 1) * KP].rearrange("(p j) c -> p j c", j=PACK)
+            )
+            return t
+
+        def gather_words(a):
+            nc.vector.tensor_copy(out=picked[a][:], in_=tab_sb[a][:].bitcast(U32).indirect(offs_sb[:]))
+
+        def quantise(src, width, name):
+            codes = keep.tile([P, width // PACK], U32, name=name + "_codes", align_bytes=64)
+            plane = keep.tile([P, width // PACK], U8, name=name + "_plane", align_bytes=64)
+            nc.vector.quantize_mx(out=codes[:].bitcast(FP8X4), scales=plane[:], in_=src)
+            return codes, plane
+
+        def round_w1(t, copies):
+            r = rounded.tile([P, PACK * KP], BF16, name="rounded", align_bytes=64)
+            for i, copy in enumerate(copies):
+                q = slice(i * P // 2, (i + 1) * P // 2)
+                copy(
+                    out=r[:].rearrange("p (t q j) -> p q j t", t=PACK, j=PACK)[:, q],
+                    in_=t[:].rearrange("p j (q t) -> p q j t", t=PACK)[:, q],
+                )
+            return r
+
+        def slots(w1q):
+            return [(w1q[0][:, t * P : (t + 1) * P], w1q[1][:, t * P : (t + 1) * P]) for t in range(w1q[0].shape[1] // P)]
+
+        def first_product(w1_slots):
+            banks = []
+            for t in range(PACK):
+                pair = [psum.tile([P, BANK], F32, name="bank") for half in range(S // BANK)]
+                for a in range(K_PASSES):
+                    codes, plane = w1_slots[a][t]
+                    for half in range(S // BANK):
+                        cols = slice(half * BANK, (half + 1) * BANK)
+                        nc.tensor.matmul_mx(
+                            out=pair[half][:],
+                            lhsT=codes.bitcast(FP8X4),
+                            lhsT_scale=plane,
+                            rhs=picked[a][:, cols].bitcast(FP8X4),
+                            rhs_scale=picked_plane[PLANE_ROW[a] : P, cols],
+                            start=(a == 0),
+                            stop=(a == K_PASSES - 1),
+                        )
+                banks.append(pair)
+            return banks
+
+        on_scalar = (nc.scalar.copy, nc.scalar.copy)
+        shared = (nc.scalar.copy, nc.vector.tensor_copy)
+
+        nc.sync.dma_start(offs_sb[:], offs)
+        nc.sync.dma_start(out=gain_sb[:], in_=gain.rearrange("(b p t) -> p b t", b=H_PASSES, t=PACK))
+        w1_raw = {}
+        w1_raw[0, 0] = load_w1(0, 0)
+        for s in range(2):
+            nc.sync.dma_start(
+                out=tab_rows[s:P:8, :], in_=tab_scales[0:2, s:16:2, :].rearrange("a g c -> g a c").bitcast(I32)
+            )
+            nc.sync.dma_start(out=tab_rows[4 + s : P : 16, :], in_=tab_scales[2, s:16:2, :].bitcast(I32))
+        load_words(0)
+        w1_raw[1, 0] = load_w1(1, 0)
+        load_words(1)
+        load_words(2)
+        w1_raw[2, 0] = load_w1(2, 0)
+        nc.sync.dma_start(out=b1_sb[:], in_=b1.rearrange("(b p t) -> p b t", b=H_PASSES, t=PACK))
+        nc.sync.dma_start(pos1_sb[:], pos1)
+        nc.sync.dma_start(pos2_sb[:], pos2)
+
+        def spread_gain(b):
+            g = keep.tile([P, PACK, PAIRS], F32, name=f"gains{b}")
+            nc.scalar.copy(out=g[:], in_=gain_sb[:, b, :].unsqueeze(2).to_broadcast([P, PACK, PAIRS]))
+            return g
+
+        gains = [spread_gain(0)]
+        nc.vector.tensor_copy(out=picked_rows[:], in_=tab_rows[:].bitcast(U8).indirect(offs_sb[:]))
+        nc.vector.tensor_copy(out=picked_plane[:].bitcast(I32), in_=picked_rows[:].bitcast(I32))
+        for s in range(2):
+            nc.gpsimd.dma_start(
+                out=picked_plane[2 + s : P - 16 : 4, :].bitcast(I32), in_=picked_rows[16 + s : P : 4, :].bitcast(I32)
+            )
+
+        def features(banks, b, evening, morning):
+            for t in range(PACK):
+                h = feat.tile([P, S], F32, name="feat")
+                for half in range(S // BANK):
+                    nc.scalar.activation(
+                        out=h[:, half * BANK : (half + 1) * BANK],
+                        in_=banks[t][half][:],
+                        func=ACT.Gelu_apprx_tanh,
+                        bias=b1_sb[:, b, t : t + 1],
+                    )
+                nc.vector.tensor_tensor(evening[:, t, :], h[:].indirect(pos1_sb[:]), gains[b][:, t, :], ALU.mult)
+                nc.vector.tensor_tensor(morning[:, t, :], h[:].indirect(pos2_sb[:]), gains[b][:, t, :], ALU.mult)
+
+        def by_lines(tile3, cols):
+            return tile3[:, :, cols].rearrange("p t (c i) -> p c t i", i=PACK)
+
+        def woven(flat):
+            return flat.rearrange("p (c i t) -> p c t i", i=PACK, t=PACK)
+
+        evening = [keep.tile([P, PACK, PAIRS], F32, name=f"evening{b}") for b in range(H_PASSES)]
+        x_bf = [keep.tile([P, PACK * PAIRS], BF16, name=f"x_bf{b}", align_bytes=64) for b in range(H_PASSES)]
+
+        w1_slots = []
+        for a in range(K_PASSES - 1):
+            gather_words(a)
+            w1_slots.append(slots(quantise(round_w1(w1_raw[a, 0], on_scalar)[:], PACK * KP, f"w1_{a}0")))
+        gains.append(spread_gain(1))
+        gather_words(K_PASSES - 1)
+        last = round_w1(w1_raw[K_PASSES - 1, 0], shared)
+        w1_slots.append(slots(quantise(last[:, :KP], KP, "w1_first")) + slots(quantise(last[:, KP:], 3 * KP, "w1_rest")))
+        banks = first_product(w1_slots)
+        for a in range(K_PASSES):
+            w1_raw[a, 1] = load_w1(a, 1)
+        nc.sync.dma_start(
+            out=w2_raw[:].bitcast(I32), in_=w2_words.rearrange("a p c -> p a c").bitcast(I32)
+        )
+        for r in range(4):
+            nc.sync.dma_start(
+                out=w2_raw_plane[r:P:32, :, :].bitcast(I32),
+                in_=w2_scales[:, r:16:4, :].rearrange("a q c -> q a c").bitcast(I32),
+            )
+        morning = keep.tile([P, PACK, PAIRS], F32, name="morning")
+        features(banks, 0, evening[0], morning)
+
+        banks = first_product(
+            [slots(quantise(round_w1(w1_raw[a, 1], on_scalar)[:], PACK * KP, f"w1_{a}1")) for a in range(K_PASSES)]
+        )
+        w3_raw = []
+        for b in range(H_PASSES):
+            t = raw.tile([P, PACK, N], F32, name="raw")
+            nc.sync.dma_start(out=t[:], in_=w3[b * KP : (b + 1) * KP, :].rearrange("(p j) n -> p j n", j=PACK))
+            w3_raw.append(t)
+        with nc.allow_non_contiguous_dma(reason="one bias value a partition"):
+            nc.sync.dma_start(out=b3_sb[:], in_=b3.rearrange("(c p) -> p c", p=P))
+
+        everything = slice(0, PAIRS)
+        nc.vector.tensor_tensor(
+            woven(x_bf[0][:]), by_lines(evening[0], everything), by_lines(morning, everything), ALU.subtract
+        )
+        x_q0 = quantise(x_bf[0][:], PACK * PAIRS, "x0")
+
+        morning = keep.tile([P, PACK, PAIRS], F32, name="morning")
+        features(banks, 1, evening[1], morning)
+
+        nc.scalar.copy(
+            out=w2_codes[:].rearrange("p a (b t q) -> p (a b) q t", t=PACK, q=P),
+            in_=w2_raw[:].rearrange("p a (b q t) -> p (a b) q t", t=PACK, q=P),
+        )
+        nc.vector.tensor_copy(
+            out=w2_plane[:].rearrange("p a (b t q) -> p (a b) q t", t=PACK, q=P),
+            in_=w2_raw_plane[:].rearrange("p a (b q t) -> p (a b) q t", t=PACK, q=P),
+        )
+        w3_q = []
+        for b in range(H_PASSES):
+            r = rounded.tile([P, PACK * N], BF16, name="rounded", align_bytes=64)
+            nc.scalar.copy(out=woven(r[:]), in_=by_lines(w3_raw[b], slice(0, N)))
+            w3_q.append(quantise(r[:], PACK * N, f"w3_{b}"))
+
+        quarters = range(PAIRS // QUARTER)
+        x_q1 = []
+        for u in quarters:
+            cols = slice(u * QUARTER, (u + 1) * QUARTER)
+            flat = x_bf[1][:, u * KP : (u + 1) * KP]
+            nc.vector.tensor_tensor(woven(flat), by_lines(evening[1], cols), by_lines(morning, cols), ALU.subtract)
+        for u in quarters:
+            x_q1.append(quantise(x_bf[1][:, u * KP : (u + 1) * KP], KP, f"x1_{u}"))
+
+        z_bf = []
+        for u in quarters:
+            cols = slice(u * QUARTER, (u + 1) * QUARTER)
+            z = keep.tile([P, H_PASSES, KP], BF16, name=f"z_bf{u}", align_bytes=64)
+            for b in range(H_PASSES):
+                y = psum.tile([P, PACK, QUARTER], F32, name="bank")
+                for t in range(PACK):
+                    m = slice(b * KP + t * P, b * KP + (t + 1) * P)
+                    for a in range(H_PASSES):
+                        x_codes, x_plane = (x_q0[0][:, cols], x_q0[1][:, cols]) if a == 0 else (x_q1[u][0][:], x_q1[u][1][:])
+                        nc.tensor.matmul_mx(
+                            out=y[:, t, :],
+                            lhsT=w2_codes[:, a, m].bitcast(FP4X4),
+                            lhsT_scale=w2_plane[:, a, m],
+                            rhs=x_codes.bitcast(FP8X4),
+                            rhs_scale=x_plane,
+                            start=(a == 0),
+                            stop=(a == H_PASSES - 1),
+                        )
+                nc.vector.tensor_tensor(
+                    woven(z[:, b, :]), by_lines(y, slice(0, QUARTER)), by_lines(evening[b], cols), ALU.max
+                )
+            z_bf.append(z)
+
+        for u in quarters:
+            cols = slice(u * QUARTER, (u + 1) * QUARTER)
+            z_codes, z_plane = quantise(z_bf[u][:].rearrange("p b c -> p (b c)"), H_PASSES * KP, f"z{u}")
+            acc = psum.tile([P, N_TILES, QUARTER], F32, name="bank")
+            res = keep.tile([P, N_TILES, QUARTER], F32, name=f"res{u}")
+            for c in range(N_TILES):
+                n = slice(c * P, (c + 1) * P)
+                for b in range(H_PASSES):
+                    nc.tensor.matmul_mx(
+                        out=acc[:, c, :],
+                        lhsT=w3_q[b][0][:, n].bitcast(FP8X4),
+                        lhsT_scale=w3_q[b][1][:, n],
+                        rhs=z_codes[:, b * QUARTER : (b + 1) * QUARTER].bitcast(FP8X4),
+                        rhs_scale=z_plane[:, b * QUARTER : (b + 1) * QUARTER],
+                        start=(b == 0),
+                        stop=(b == H_PASSES - 1),
+                    )
+            for c in range(N_TILES):
+                nc.scalar.activation(
+                    out=res[:, c, :], in_=acc[:, c, :], func=ACT.Identity, bias=b3_sb[:, c : c + 1]
+                )
+            nc.sync.dma_start(out=out[:, cols].rearrange("(c p) j -> p c j", p=P), in_=res[:])

@@ -24,6 +24,7 @@ K_PASSES = K // KP
 H_PASSES = H // KP
 N_TILES = N // P
 QUARTER = 128
+HALF = 256
 PLANE_ROW = (0, 8, 4)
 
 
@@ -33,68 +34,70 @@ def tile_list_udder_health_watch_kernel(
     nc = tc.nc
     with ExitStack() as ctx:
         keep = ctx.enter_context(tc.tile_pool(name="keep", bufs=1))
-        raw = ctx.enter_context(tc.tile_pool(name="raw", bufs=4))
+        stage = ctx.enter_context(tc.tile_pool(name="stage", bufs=1))
         rounded = ctx.enter_context(tc.tile_pool(name="rounded", bufs=3))
-        feat = ctx.enter_context(tc.tile_pool(name="feat", bufs=6))
+        feat = ctx.enter_context(tc.tile_pool(name="feat", bufs=8))
+        act = ctx.enter_context(tc.tile_pool(name="act", bufs=3))
         psum = ctx.enter_context(tc.psum_pool(name="psum", bufs=8))
 
         offs_sb = keep.tile([P, S // 16], U16, name="offs_sb")
         pos1_sb = keep.tile([P, PAIRS // 16], U16, name="pos1_sb")
         pos2_sb = keep.tile([P, PAIRS // 16], U16, name="pos2_sb")
-        tab_sb = [keep.tile([P, T], I32, name=f"tab{a}") for a in range(K_PASSES)]
-        tab_rows = keep.tile([P, T // 4], I32, name="tab_rows")
         picked = [keep.tile([P, S], U32, name=f"picked{a}", align_bytes=64) for a in range(K_PASSES)]
         picked_rows = keep.tile([P, S], U8, name="picked_rows", align_bytes=64)
         picked_plane = keep.tile([P, S], U8, name="picked_plane", align_bytes=64)
         b1_sb = keep.tile([P, H_PASSES, PACK], F32, name="b1_sb")
         gain_sb = keep.tile([P, H_PASSES, PACK], F32, name="gain_sb")
-        b3_sb = keep.tile([P, N_TILES], F32, name="b3_sb")
-        w2_raw = keep.tile([P, H_PASSES, H], U16, name="w2_raw")
-        w2_raw_plane = keep.tile([P, H_PASSES, H], U8, name="w2_raw_plane")
         w2_codes = keep.tile([P, H_PASSES, H], U16, name="w2_codes", align_bytes=64)
-        w2_plane = keep.tile([P, H_PASSES, H], U8, name="w2_plane", align_bytes=64)
+        evening = [keep.tile([P, PACK, PAIRS], F32, name=f"evening{b}") for b in range(H_PASSES)]
+        minus_x = [keep.tile([P, PACK, PAIRS], F32, name=f"minus_x{b}") for b in range(H_PASSES)]
 
-        nc.vector.memset(tab_rows[:], 0)
-        nc.vector.memset(w2_raw_plane[:].rearrange("p a c -> p (a c)").bitcast(I32), 0)
+        def staged(slot, shape, dtype):
+            return stage.tile(shape, dtype, name=f"stage{slot}")
 
-        def load_words(a):
-            nc.sync.dma_start(out=tab_sb[a][:], in_=tab_words[a].rearrange("p t i -> p (t i)").bitcast(I32))
-
-        def load_w1(a, b):
-            t = raw.tile([P, PACK, KP], F32, name="raw")
-            nc.sync.dma_start(
-                out=t[:], in_=w1[a * KP : (a + 1) * KP, b * KP : (b + 1) * KP].rearrange("(p j) c -> p j c", j=PACK)
-            )
+        def load_words(a, slot):
+            t = staged(slot, [P, T], I32)
+            nc.sync.dma_start(out=t[:], in_=tab_words[a].rearrange("p t i -> p (t i)").bitcast(I32))
             return t
 
-        def gather_words(a):
-            nc.vector.tensor_copy(out=picked[a][:], in_=tab_sb[a][:].bitcast(U32).indirect(offs_sb[:]))
+        def w1_rows(a, cols):
+            return w1[a * KP : (a + 1) * KP, cols].rearrange("(p j) c -> p j c", j=PACK)
 
-        def quantise(src, width, name):
-            codes = keep.tile([P, width // PACK], U32, name=name + "_codes", align_bytes=64)
-            plane = keep.tile([P, width // PACK], U8, name=name + "_plane", align_bytes=64)
+        def load_w1(a, cols, slot):
+            t = staged(slot, [P, PACK, KP], F32)
+            nc.sync.dma_start(out=t[:], in_=w1_rows(a, cols))
+            return [t[:, :, :HALF], t[:, :, HALF:]]
+
+        def load_w1_halves(a, slot):
+            t = staged(slot, [P, 2, PACK, HALF], F32)
+            for i in range(2):
+                nc.sync.dma_start(out=t[:, i], in_=w1_rows(a, slice(i * HALF, (i + 1) * HALF)))
+            return [t[:, 0], t[:, 1]]
+
+        def quantise(src, name, after=None):
+            words = src.shape[1] // PACK
+            codes = keep.tile([P, words], U32, name=after or name + "_codes", align_bytes=64)
+            plane = keep.tile([P, words], U8, name=name + "_plane", align_bytes=64)
             nc.vector.quantize_mx(out=codes[:].bitcast(FP8X4), scales=plane[:], in_=src)
-            return codes, plane
+            return [(codes[:, c : c + P], plane[:, c : c + P]) for c in range(0, words, P)]
 
-        def round_w1(t, copies):
-            r = rounded.tile([P, PACK * KP], BF16, name="rounded", align_bytes=64)
+        def round_w1(parts, copies, r):
             for i, copy in enumerate(copies):
-                q = slice(i * P // 2, (i + 1) * P // 2)
                 copy(
-                    out=r[:].rearrange("p (t q j) -> p q j t", t=PACK, j=PACK)[:, q],
-                    in_=t[:].rearrange("p j (q t) -> p q j t", t=PACK)[:, q],
+                    out=r[:].rearrange("p (t q j) -> p q j t", t=PACK, j=PACK)[:, i * P // 2 : (i + 1) * P // 2],
+                    in_=parts[i].rearrange("p j (q t) -> p q j t", t=PACK),
                 )
             return r
 
-        def slots(w1q):
-            return [(w1q[0][:, t * P : (t + 1) * P], w1q[1][:, t * P : (t + 1) * P]) for t in range(w1q[0].shape[1] // P)]
+        def new_rounded(width):
+            return rounded.tile([P, width], BF16, name="rounded", align_bytes=64)
 
-        def first_product(w1_slots):
+        def first_product(w1_q):
             banks = []
             for t in range(PACK):
                 pair = [psum.tile([P, BANK], F32, name="bank") for half in range(S // BANK)]
                 for a in range(K_PASSES):
-                    codes, plane = w1_slots[a][t]
+                    codes, plane = w1_q[a][t]
                     for half in range(S // BANK):
                         cols = slice(half * BANK, (half + 1) * BANK)
                         nc.tensor.matmul_mx(
@@ -109,52 +112,22 @@ def tile_list_udder_health_watch_kernel(
                 banks.append(pair)
             return banks
 
-        on_scalar = (nc.scalar.copy, nc.scalar.copy)
-        shared = (nc.scalar.copy, nc.vector.tensor_copy)
-
-        nc.sync.dma_start(offs_sb[:], offs)
-        nc.sync.dma_start(out=gain_sb[:], in_=gain.rearrange("(b p t) -> p b t", b=H_PASSES, t=PACK))
-        w1_raw = {}
-        w1_raw[0, 0] = load_w1(0, 0)
-        for s in range(2):
-            nc.sync.dma_start(
-                out=tab_rows[s:P:8, :], in_=tab_scales[0:2, s:16:2, :].rearrange("a g c -> g a c").bitcast(I32)
-            )
-            nc.sync.dma_start(out=tab_rows[4 + s : P : 16, :], in_=tab_scales[2, s:16:2, :].bitcast(I32))
-        load_words(0)
-        w1_raw[1, 0] = load_w1(1, 0)
-        load_words(1)
-        load_words(2)
-        w1_raw[2, 0] = load_w1(2, 0)
-        nc.sync.dma_start(out=b1_sb[:], in_=b1.rearrange("(b p t) -> p b t", b=H_PASSES, t=PACK))
-        nc.sync.dma_start(pos1_sb[:], pos1)
-        nc.sync.dma_start(pos2_sb[:], pos2)
-
-        def spread_gain(b):
-            g = keep.tile([P, PACK, PAIRS], F32, name=f"gains{b}")
-            nc.scalar.copy(out=g[:], in_=gain_sb[:, b, :].unsqueeze(2).to_broadcast([P, PACK, PAIRS]))
-            return g
-
-        gains = [spread_gain(0)]
-        nc.vector.tensor_copy(out=picked_rows[:], in_=tab_rows[:].bitcast(U8).indirect(offs_sb[:]))
-        nc.vector.tensor_copy(out=picked_plane[:].bitcast(I32), in_=picked_rows[:].bitcast(I32))
-        for s in range(2):
-            nc.gpsimd.dma_start(
-                out=picked_plane[2 + s : P - 16 : 4, :].bitcast(I32), in_=picked_rows[16 + s : P : 4, :].bitcast(I32)
-            )
-
-        def features(banks, b, evening, morning):
-            for t in range(PACK):
-                h = feat.tile([P, S], F32, name="feat")
-                for half in range(S // BANK):
-                    nc.scalar.activation(
-                        out=h[:, half * BANK : (half + 1) * BANK],
-                        in_=banks[t][half][:],
-                        func=ACT.Gelu_apprx_tanh,
-                        bias=b1_sb[:, b, t : t + 1],
-                    )
-                nc.vector.tensor_tensor(evening[:, t, :], h[:].indirect(pos1_sb[:]), gains[b][:, t, :], ALU.mult)
-                nc.vector.tensor_tensor(morning[:, t, :], h[:].indirect(pos2_sb[:]), gains[b][:, t, :], ALU.mult)
+        def feature(banks, b, t, g=None, piece=HALF):
+            if g is None:
+                g = act.tile([P, S], F32, name="gelu")
+            h = feat.tile([P, S], F32, name="feat")
+            for half in range(S // BANK):
+                cols = slice(half * BANK, (half + 1) * BANK)
+                nc.scalar.activation(
+                    out=g[:, cols], in_=banks[t][half][:], func=ACT.Gelu_apprx_tanh, bias=b1_sb[:, b, t : t + 1]
+                )
+                nc.gpsimd.tensor_scalar(h[:, cols], g[:, cols], gain_sb[:, b, t : t + 1], 0.0, ALU.mult, ALU.add)
+            for c in range(0, PAIRS, piece):
+                cols, entries = slice(c, c + piece), slice(c // 16, (c + piece) // 16)
+                nc.vector.tensor_copy(out=evening[b][:, t, cols], in_=h[:].indirect(pos1_sb[:, entries]))
+                nc.vector.tensor_tensor(
+                    minus_x[b][:, t, cols], h[:].indirect(pos2_sb[:, entries]), evening[b][:, t, cols], ALU.subtract
+                )
 
         def by_lines(tile3, cols):
             return tile3[:, :, cols].rearrange("p t (c i) -> p c t i", i=PACK)
@@ -162,117 +135,158 @@ def tile_list_udder_health_watch_kernel(
         def woven(flat):
             return flat.rearrange("p (c i t) -> p c t i", i=PACK, t=PACK)
 
-        evening = [keep.tile([P, PACK, PAIRS], F32, name=f"evening{b}") for b in range(H_PASSES)]
-        x_bf = [keep.tile([P, PACK * PAIRS], BF16, name=f"x_bf{b}", align_bytes=64) for b in range(H_PASSES)]
+        def round_x(b, cols):
+            flat = keep.tile([P, PACK * (cols.stop - cols.start)], BF16, name=f"x{b}_{cols.start}", align_bytes=64)
+            nc.scalar.activation(out=woven(flat[:]), in_=by_lines(minus_x[b], cols), func=ACT.Copy, scale=-1.0)
+            return flat[:]
 
-        w1_slots = []
-        for a in range(K_PASSES - 1):
-            gather_words(a)
-            w1_slots.append(slots(quantise(round_w1(w1_raw[a, 0], on_scalar)[:], PACK * KP, f"w1_{a}0")))
-        gains.append(spread_gain(1))
-        gather_words(K_PASSES - 1)
-        last = round_w1(w1_raw[K_PASSES - 1, 0], shared)
-        w1_slots.append(slots(quantise(last[:, :KP], KP, "w1_first")) + slots(quantise(last[:, KP:], 3 * KP, "w1_rest")))
-        banks = first_product(w1_slots)
-        for a in range(K_PASSES):
-            w1_raw[a, 1] = load_w1(a, 1)
-        nc.sync.dma_start(
-            out=w2_raw[:].bitcast(I32), in_=w2_words.rearrange("a p c -> p a c").bitcast(I32)
-        )
+        def deal(tile2):
+            return tile2.rearrange("p (g t q) -> p g q t", t=PACK, q=P)
+
+        def undealt(tile2):
+            return tile2.rearrange("p (g q t) -> p g q t", t=PACK, q=P)
+
+        on_scalar = (nc.scalar.copy, nc.scalar.copy)
+        shared = (nc.scalar.copy, nc.vector.tensor_copy)
+        lower, upper = slice(0, KP), slice(KP, H)
+
+        nc.vector.memset(picked_plane[:].bitcast(I32), 0)
+        nc.sync.dma_start(offs_sb[:], offs)
+        nc.sync.dma_start(pos1_sb[:], pos1)
+        nc.sync.dma_start(pos2_sb[:], pos2)
+        nc.sync.dma_start(out=b1_sb[:], in_=b1.rearrange("(b p t) -> p b t", b=H_PASSES, t=PACK))
+        nc.sync.dma_start(out=gain_sb[:], in_=gain.rearrange("(b p t) -> p b t", b=H_PASSES, t=PACK))
+        w1_lower0 = load_w1(0, lower, 0)
+        tab_rows = staged(1, [P, T // 4], I32)
+        nc.gpsimd.memset(tab_rows[:], 0)
+        for s in range(2):
+            nc.sync.dma_start(
+                out=tab_rows[s:P:8, :], in_=tab_scales[0:2, s:16:2, :].rearrange("a g c -> g a c").bitcast(I32)
+            )
+            nc.sync.dma_start(out=tab_rows[4 + s : P : 16, :], in_=tab_scales[2, s:16:2, :].bitcast(I32))
+        tab_sb = [load_words(a, 2 + a) for a in range(K_PASSES)]
+
+        nc.vector.tensor_copy(out=picked_rows[:], in_=tab_rows[:].bitcast(U8).indirect(offs_sb[:]))
+        for s in range(2):
+            nc.sync.dma_start(out=picked_plane[s:P:4, :].bitcast(I32), in_=picked_rows[s:P:4, :].bitcast(I32))
+            nc.sync.dma_start(
+                out=picked_plane[2 + s : P - 16 : 4, :].bitcast(I32), in_=picked_rows[16 + s : P : 4, :].bitcast(I32)
+            )
+        w1_lower1 = load_w1_halves(1, 1)
+        w1_lower2 = load_w1_halves(2, 0)
+        w2_raw_plane = staged(2, [P, H_PASSES * H], U8)
+        nc.gpsimd.memset(w2_raw_plane[:].bitcast(I32), 0)
         for r in range(4):
             nc.sync.dma_start(
-                out=w2_raw_plane[r:P:32, :, :].bitcast(I32),
+                out=w2_raw_plane[r:P:32, :].rearrange("q (a c) -> q a c", a=H_PASSES).bitcast(I32),
                 in_=w2_scales[:, r:16:4, :].rearrange("a q c -> q a c").bitcast(I32),
             )
-        morning = keep.tile([P, PACK, PAIRS], F32, name="morning")
-        features(banks, 0, evening[0], morning)
 
-        banks = first_product(
-            [slots(quantise(round_w1(w1_raw[a, 1], on_scalar)[:], PACK * KP, f"w1_{a}1")) for a in range(K_PASSES)]
-        )
+        w1_q = [quantise(round_w1(w1_lower0, on_scalar, new_rounded(PACK * KP))[:], "w1_lower0")]
+        for a in range(K_PASSES):
+            nc.vector.tensor_copy(out=picked[a][:], in_=tab_sb[a][:].bitcast(U32).indirect(offs_sb[:]))
+        r1 = round_w1(w1_lower1, shared, new_rounded(PACK * KP))
+        first1 = quantise(r1[:, :KP], "w1_first1")
+        r2 = keep.tile([P, PACK * KP], BF16, name="last", align_bytes=64)
+        round_w1(w1_lower2, shared, r2)
+        first2 = quantise(r2[:, :KP], "w1_first2")
+        w1_q.append(first1 + quantise(r1[:, KP:], "w1_rest1"))
+        w1_q.append(first2 + quantise(r2[:, KP:], "w1_rest2"))
+        banks = first_product(w1_q)
+        w2_plane = keep.tile([P, H_PASSES * H], U8, name="last", align_bytes=64)
+        nc.vector.tensor_copy(out=deal(w2_plane[:]), in_=undealt(w2_raw_plane[:]))
+
+        w1_upper = [load_w1(a, upper, slot) for a, slot in enumerate((3, 4, 1))]
+        w2_raw = staged(0, [P, H_PASSES, H], U16)
+        nc.sync.dma_start(out=w2_raw[:].bitcast(I32), in_=w2_words.rearrange("a p c -> p a c").bitcast(I32))
+
+        def upper_w1(a, copies):
+            return quantise(round_w1(w1_upper[a], copies, new_rounded(PACK * KP))[:], f"w1_upper{a}")
+
+        feature(banks, 0, 0)
+        w1_q = [upper_w1(0, on_scalar)]
+        feature(banks, 0, 1, staged(3, [P, S], F32))
+        w1_q.append(upper_w1(1, on_scalar))
+        feature(banks, 0, 2, staged(4, [P, S], F32))
+        w1_q.append(upper_w1(2, shared))
+        feature(banks, 0, 3, staged(1, [P, S], F32))
+
+        for a in range(H_PASSES):
+            for cols in (lower, upper):
+                nc.scalar.copy(out=deal(w2_codes[:, a, cols]), in_=undealt(w2_raw[:, a, cols]))
+
         w3_raw = []
-        for b in range(H_PASSES):
-            t = raw.tile([P, PACK, N], F32, name="raw")
+        for b, slot in enumerate((3, 2)):
+            t = staged(slot, [P, PACK, N], F32)
             nc.sync.dma_start(out=t[:], in_=w3[b * KP : (b + 1) * KP, :].rearrange("(p j) n -> p j n", j=PACK))
             w3_raw.append(t)
+        b3_sb = staged(4, [P, N_TILES], F32)
         with nc.allow_non_contiguous_dma(reason="one bias value a partition"):
             nc.sync.dma_start(out=b3_sb[:], in_=b3.rearrange("(c p) -> p c", p=P))
 
-        everything = slice(0, PAIRS)
-        nc.vector.tensor_tensor(
-            woven(x_bf[0][:]), by_lines(evening[0], everything), by_lines(morning, everything), ALU.subtract
-        )
-        x_q0 = quantise(x_bf[0][:], PACK * PAIRS, "x0")
+        banks = first_product(w1_q)
+        feature(banks, 1, 0)
+        feature(banks, 1, 1)
+        x_q = [quantise(round_x(0, slice(0, HALF)), "x0_left")]
+        feature(banks, 1, 2)
+        x_q[0] = x_q[0] + quantise(round_x(0, slice(HALF, PAIRS)), "x0_right")
+        feature(banks, 1, 3, piece=QUARTER)
 
-        morning = keep.tile([P, PACK, PAIRS], F32, name="morning")
-        features(banks, 1, evening[1], morning)
-
-        nc.scalar.copy(
-            out=w2_codes[:].rearrange("p a (b t q) -> p (a b) q t", t=PACK, q=P),
-            in_=w2_raw[:].rearrange("p a (b q t) -> p (a b) q t", t=PACK, q=P),
-        )
-        nc.vector.tensor_copy(
-            out=w2_plane[:].rearrange("p a (b t q) -> p (a b) q t", t=PACK, q=P),
-            in_=w2_raw_plane[:].rearrange("p a (b q t) -> p (a b) q t", t=PACK, q=P),
-        )
+        quarters = [slice(c, c + QUARTER) for c in range(0, PAIRS, QUARTER)]
+        x_q.append([quantise(round_x(1, cols), f"x1_{u}")[0] for u, cols in enumerate(quarters)])
         w3_q = []
         for b in range(H_PASSES):
-            r = rounded.tile([P, PACK * N], BF16, name="rounded", align_bytes=64)
+            r = new_rounded(PACK * N)
             nc.scalar.copy(out=woven(r[:]), in_=by_lines(w3_raw[b], slice(0, N)))
-            w3_q.append(quantise(r[:], PACK * N, f"w3_{b}"))
+            w3_q.append(quantise(r[:], f"w3_{b}", after=f"x1_{quarters[b].start}"))
 
-        quarters = range(PAIRS // QUARTER)
-        x_q1 = []
-        for u in quarters:
-            cols = slice(u * QUARTER, (u + 1) * QUARTER)
-            flat = x_bf[1][:, u * KP : (u + 1) * KP]
-            nc.vector.tensor_tensor(woven(flat), by_lines(evening[1], cols), by_lines(morning, cols), ALU.subtract)
-        for u in quarters:
-            x_q1.append(quantise(x_bf[1][:, u * KP : (u + 1) * KP], KP, f"x1_{u}"))
-
-        z_bf = []
-        for u in quarters:
-            cols = slice(u * QUARTER, (u + 1) * QUARTER)
-            z = keep.tile([P, H_PASSES, KP], BF16, name=f"z_bf{u}", align_bytes=64)
-            for b in range(H_PASSES):
-                y = psum.tile([P, PACK, QUARTER], F32, name="bank")
-                for t in range(PACK):
-                    m = slice(b * KP + t * P, b * KP + (t + 1) * P)
-                    for a in range(H_PASSES):
-                        x_codes, x_plane = (x_q0[0][:, cols], x_q0[1][:, cols]) if a == 0 else (x_q1[u][0][:], x_q1[u][1][:])
-                        nc.tensor.matmul_mx(
-                            out=y[:, t, :],
-                            lhsT=w2_codes[:, a, m].bitcast(FP4X4),
-                            lhsT_scale=w2_plane[:, a, m],
-                            rhs=x_codes.bitcast(FP8X4),
-                            rhs_scale=x_plane,
-                            start=(a == 0),
-                            stop=(a == H_PASSES - 1),
-                        )
-                nc.vector.tensor_tensor(
-                    woven(z[:, b, :]), by_lines(y, slice(0, QUARTER)), by_lines(evening[b], cols), ALU.max
+        def second_pass(y, u, b, a):
+            x_codes, x_plane = x_q[a][u]
+            for t in range(PACK):
+                m = b * KP + t * P
+                nc.tensor.matmul_mx(
+                    out=y[:, t, :],
+                    lhsT=w2_codes[:, a, m : m + P].bitcast(FP4X4),
+                    lhsT_scale=w2_plane[:, a * H + m : a * H + m + P],
+                    rhs=x_codes.bitcast(FP8X4),
+                    rhs_scale=x_plane,
+                    start=(a == 0 and t == 0),
+                    stop=(a == H_PASSES - 1 and t == PACK - 1),
                 )
-            z_bf.append(z)
 
-        for u in quarters:
-            cols = slice(u * QUARTER, (u + 1) * QUARTER)
-            z_codes, z_plane = quantise(z_bf[u][:].rearrange("p b c -> p (b c)"), H_PASSES * KP, f"z{u}")
-            acc = psum.tile([P, N_TILES, QUARTER], F32, name="bank")
+        def third_pass(acc, u, b):
+            z_codes, z_plane = quantise(z_bf[u, b][:], f"z{u}{b}")[0]
+            for c in range(N_TILES):
+                nc.tensor.matmul_mx(
+                    out=acc[:, c, :],
+                    lhsT=w3_q[b][c][0].bitcast(FP8X4),
+                    lhsT_scale=w3_q[b][c][1],
+                    rhs=z_codes.bitcast(FP8X4),
+                    rhs_scale=z_plane,
+                    start=(b == 0 and c == 0),
+                    stop=(b == H_PASSES - 1 and c == N_TILES - 1),
+                )
+
+        def store(acc, u):
             res = keep.tile([P, N_TILES, QUARTER], F32, name=f"res{u}")
             for c in range(N_TILES):
-                n = slice(c * P, (c + 1) * P)
-                for b in range(H_PASSES):
-                    nc.tensor.matmul_mx(
-                        out=acc[:, c, :],
-                        lhsT=w3_q[b][0][:, n].bitcast(FP8X4),
-                        lhsT_scale=w3_q[b][1][:, n],
-                        rhs=z_codes[:, b * QUARTER : (b + 1) * QUARTER].bitcast(FP8X4),
-                        rhs_scale=z_plane[:, b * QUARTER : (b + 1) * QUARTER],
-                        start=(b == 0),
-                        stop=(b == H_PASSES - 1),
-                    )
-            for c in range(N_TILES):
-                nc.scalar.activation(
-                    out=res[:, c, :], in_=acc[:, c, :], func=ACT.Identity, bias=b3_sb[:, c : c + 1]
+                nc.scalar.activation(out=res[:, c, :], in_=acc[:, c, :], func=ACT.Identity, bias=b3_sb[:, c : c + 1])
+            nc.sync.dma_start(out=out[:, quarters[u]].rearrange("(c p) j -> p c j", p=P), in_=res[:])
+
+        ys = {}
+        for u in range(len(quarters)):
+            for b in range(H_PASSES):
+                ys[u, b] = psum.tile([P, PACK, QUARTER], F32, name="bank")
+                second_pass(ys[u, b], u, b, 0)
+        z_bf = {}
+        for u, cols in enumerate(quarters):
+            for b in range(H_PASSES):
+                second_pass(ys[u, b], u, b, 1)
+                z_bf[u, b] = keep.tile([P, KP], BF16, name=f"z_bf{u}{b}", align_bytes=64)
+                nc.vector.tensor_tensor(
+                    woven(z_bf[u, b][:]), by_lines(ys[u, b], slice(0, QUARTER)), by_lines(evening[b], cols), ALU.max
                 )
-            nc.sync.dma_start(out=out[:, cols].rearrange("(c p) j -> p c j", p=P), in_=res[:])
+            acc = psum.tile([P, N_TILES, QUARTER], F32, name="bank")
+            for b in range(H_PASSES):
+                third_pass(acc, u, b)
+            store(acc, u)

@@ -36,9 +36,9 @@ def tile_list_udder_health_watch_kernel(
         keep = ctx.enter_context(tc.tile_pool(name="keep", bufs=1))
         stage = ctx.enter_context(tc.tile_pool(name="stage", bufs=1))
         rounded = ctx.enter_context(tc.tile_pool(name="rounded", bufs=3))
-        feat = ctx.enter_context(tc.tile_pool(name="feat", bufs=8))
-        act = ctx.enter_context(tc.tile_pool(name="act", bufs=3))
-        psum = ctx.enter_context(tc.psum_pool(name="psum", bufs=8))
+        feat = ctx.enter_context(tc.tile_pool(name="feat", bufs=4))
+        act = ctx.enter_context(tc.tile_pool(name="act", bufs=2))
+        psum = ctx.enter_context(tc.psum_pool(name="psum", bufs=1))
 
         offs_sb = keep.tile([P, S // 16], U16, name="offs_sb")
         pos1_sb = keep.tile([P, PAIRS // 16], U16, name="pos1_sb")
@@ -50,7 +50,9 @@ def tile_list_udder_health_watch_kernel(
         gain_sb = keep.tile([P, H_PASSES, PACK], F32, name="gain_sb")
         w2_codes = keep.tile([P, H_PASSES, H], U16, name="w2_codes", align_bytes=64)
         evening = [keep.tile([P, PACK, PAIRS], F32, name=f"evening{b}") for b in range(H_PASSES)]
-        minus_x = [keep.tile([P, PACK, PAIRS], F32, name=f"minus_x{b}") for b in range(H_PASSES)]
+        morning = keep.tile([P, PACK, PAIRS], F32, name="morning")
+        minus_x = keep.tile([P, PACK, PAIRS], F32, name="minus_x")
+        gains = keep.tile([P, PACK, PAIRS], F32, name="gains")
 
         def staged(slot, shape, dtype):
             return stage.tile(shape, dtype, name=f"stage{slot}")
@@ -92,10 +94,12 @@ def tile_list_udder_health_watch_kernel(
         def new_rounded(width):
             return rounded.tile([P, width], BF16, name="rounded", align_bytes=64)
 
-        def first_product(w1_q):
-            banks = []
-            for t in range(PACK):
-                pair = [psum.tile([P, BANK], F32, name="bank") for half in range(S // BANK)]
+        def bank(i, shape):
+            return psum.tile(shape, F32, name=f"bank{i}")
+
+        def first_product(w1_q, t, where):
+            if True:
+                pair = [bank(2 * where + half, [P, BANK]) for half in range(S // BANK)]
                 for a in range(K_PASSES):
                     codes, plane = w1_q[a][t]
                     for half in range(S // BANK):
@@ -109,24 +113,35 @@ def tile_list_udder_health_watch_kernel(
                             start=(a == 0),
                             stop=(a == K_PASSES - 1),
                         )
-                banks.append(pair)
-            return banks
+            return pair
 
-        def feature(banks, b, t, g=None, piece=HALF):
-            if g is None:
-                g = act.tile([P, S], F32, name="gelu")
-            h = feat.tile([P, S], F32, name="feat")
+        def gelu(banks, b, t, g):
             for half in range(S // BANK):
-                cols = slice(half * BANK, (half + 1) * BANK)
                 nc.scalar.activation(
-                    out=g[:, cols], in_=banks[t][half][:], func=ACT.Gelu_apprx_tanh, bias=b1_sb[:, b, t : t + 1]
+                    out=g[:, half * BANK : (half + 1) * BANK],
+                    in_=banks[half][:],
+                    func=ACT.Gelu_apprx_tanh,
+                    bias=b1_sb[:, b, t : t + 1],
                 )
-                nc.gpsimd.tensor_scalar(h[:, cols], g[:, cols], gain_sb[:, b, t : t + 1], 0.0, ALU.mult, ALU.add)
+
+        def lower_feature(banks, t, g):
+            gelu(banks, 0, t, g)
+            nc.vector.tensor_tensor(evening[0][:, t, :], g[:].indirect(pos1_sb[:]), gains[:, t, :], ALU.mult)
+            nc.vector.tensor_tensor(morning[:, t, :], g[:].indirect(pos2_sb[:]), gains[:, t, :], ALU.mult)
+
+        def upper_feature(banks, t, piece):
+            g = act.tile([P, S], F32, name="gelu")
+            gelu(banks, 1, t, g)
+            h = feat.tile([P, S], F32, name="feat")
+            for c in range(0, S, BANK):
+                nc.scalar.activation(
+                    out=h[:, c : c + BANK], in_=g[:, c : c + BANK], func=ACT.Copy, scale=gain_sb[:, 1, t : t + 1]
+                )
             for c in range(0, PAIRS, piece):
                 cols, entries = slice(c, c + piece), slice(c // 16, (c + piece) // 16)
-                nc.vector.tensor_copy(out=evening[b][:, t, cols], in_=h[:].indirect(pos1_sb[:, entries]))
+                nc.vector.tensor_copy(out=evening[1][:, t, cols], in_=h[:].indirect(pos1_sb[:, entries]))
                 nc.vector.tensor_tensor(
-                    minus_x[b][:, t, cols], h[:].indirect(pos2_sb[:, entries]), evening[b][:, t, cols], ALU.subtract
+                    minus_x[:, t, cols], h[:].indirect(pos2_sb[:, entries]), evening[1][:, t, cols], ALU.subtract
                 )
 
         def by_lines(tile3, cols):
@@ -135,10 +150,15 @@ def tile_list_udder_health_watch_kernel(
         def woven(flat):
             return flat.rearrange("p (c i t) -> p c t i", i=PACK, t=PACK)
 
-        def round_x(b, cols):
-            flat = keep.tile([P, PACK * (cols.stop - cols.start)], BF16, name=f"x{b}_{cols.start}", align_bytes=64)
-            nc.scalar.activation(out=woven(flat[:]), in_=by_lines(minus_x[b], cols), func=ACT.Copy, scale=-1.0)
-            return flat[:]
+        def lower_x(cols):
+            flat = keep.tile([P, PACK * HALF], BF16, name=f"x0_{cols.start}", align_bytes=64)
+            nc.vector.tensor_tensor(woven(flat[:]), by_lines(evening[0], cols), by_lines(morning, cols), ALU.subtract)
+            return flat
+
+        def upper_x(cols):
+            flat = keep.tile([P, PACK * QUARTER], BF16, name=f"x1_{cols.start}", align_bytes=64)
+            nc.scalar.activation(out=woven(flat[:]), in_=by_lines(minus_x, cols), func=ACT.Copy, scale=-1.0)
+            return flat
 
         def deal(tile2):
             return tile2.rearrange("p (g t q) -> p g q t", t=PACK, q=P)
@@ -152,11 +172,7 @@ def tile_list_udder_health_watch_kernel(
 
         nc.vector.memset(picked_plane[:].bitcast(I32), 0)
         nc.sync.dma_start(offs_sb[:], offs)
-        nc.sync.dma_start(pos1_sb[:], pos1)
-        nc.sync.dma_start(pos2_sb[:], pos2)
-        nc.sync.dma_start(out=b1_sb[:], in_=b1.rearrange("(b p t) -> p b t", b=H_PASSES, t=PACK))
-        nc.sync.dma_start(out=gain_sb[:], in_=gain.rearrange("(b p t) -> p b t", b=H_PASSES, t=PACK))
-        w1_lower0 = load_w1(0, lower, 0)
+        tab_sb = [load_words(0, 2)]
         tab_rows = staged(1, [P, T // 4], I32)
         nc.gpsimd.memset(tab_rows[:], 0)
         for s in range(2):
@@ -164,7 +180,13 @@ def tile_list_udder_health_watch_kernel(
                 out=tab_rows[s:P:8, :], in_=tab_scales[0:2, s:16:2, :].rearrange("a g c -> g a c").bitcast(I32)
             )
             nc.sync.dma_start(out=tab_rows[4 + s : P : 16, :], in_=tab_scales[2, s:16:2, :].bitcast(I32))
-        tab_sb = [load_words(a, 2 + a) for a in range(K_PASSES)]
+        nc.sync.dma_start(out=gain_sb[:], in_=gain.rearrange("(b p t) -> p b t", b=H_PASSES, t=PACK))
+        w1_lower0 = load_w1(0, lower, 0)
+        nc.sync.dma_start(out=b1_sb[:], in_=b1.rearrange("(b p t) -> p b t", b=H_PASSES, t=PACK))
+        nc.sync.dma_start(pos1_sb[:], pos1)
+        nc.sync.dma_start(pos2_sb[:], pos2)
+        tab_sb.extend(load_words(a, 2 + a) for a in range(1, K_PASSES))
+        w1_lower1 = load_w1_halves(1, 5)
 
         nc.vector.tensor_copy(out=picked_rows[:], in_=tab_rows[:].bitcast(U8).indirect(offs_sb[:]))
         for s in range(2):
@@ -172,9 +194,8 @@ def tile_list_udder_health_watch_kernel(
             nc.sync.dma_start(
                 out=picked_plane[2 + s : P - 16 : 4, :].bitcast(I32), in_=picked_rows[16 + s : P : 4, :].bitcast(I32)
             )
-        w1_lower1 = load_w1_halves(1, 1)
-        w1_lower2 = load_w1_halves(2, 0)
-        w2_raw_plane = staged(2, [P, H_PASSES * H], U8)
+        w1_lower2 = load_w1_halves(2, 1)
+        w2_raw_plane = staged(0, [P, H_PASSES * H], U8)
         nc.gpsimd.memset(w2_raw_plane[:].bitcast(I32), 0)
         for r in range(4):
             nc.sync.dma_start(
@@ -183,6 +204,7 @@ def tile_list_udder_health_watch_kernel(
             )
 
         w1_q = [quantise(round_w1(w1_lower0, on_scalar, new_rounded(PACK * KP))[:], "w1_lower0")]
+        nc.scalar.copy(out=gains[:], in_=gain_sb[:, 0, :].unsqueeze(2).to_broadcast([P, PACK, PAIRS]))
         for a in range(K_PASSES):
             nc.vector.tensor_copy(out=picked[a][:], in_=tab_sb[a][:].bitcast(U32).indirect(offs_sb[:]))
         r1 = round_w1(w1_lower1, shared, new_rounded(PACK * KP))
@@ -192,31 +214,33 @@ def tile_list_udder_health_watch_kernel(
         first2 = quantise(r2[:, :KP], "w1_first2")
         w1_q.append(first1 + quantise(r1[:, KP:], "w1_rest1"))
         w1_q.append(first2 + quantise(r2[:, KP:], "w1_rest2"))
-        banks = first_product(w1_q)
+        lower_q = w1_q
+        banks = [first_product(lower_q, t, t) for t in range(2)]
         w2_plane = keep.tile([P, H_PASSES * H], U8, name="last", align_bytes=64)
         nc.vector.tensor_copy(out=deal(w2_plane[:]), in_=undealt(w2_raw_plane[:]))
 
-        w1_upper = [load_w1(a, upper, slot) for a, slot in enumerate((3, 4, 1))]
-        w2_raw = staged(0, [P, H_PASSES, H], U16)
+        w1_upper = [load_w1(a, upper, slot) for a, slot in enumerate((3, 4, 5))]
+        w2_raw = staged(1, [P, H_PASSES, H], U16)
         nc.sync.dma_start(out=w2_raw[:].bitcast(I32), in_=w2_words.rearrange("a p c -> p a c").bitcast(I32))
 
         def upper_w1(a, copies):
             return quantise(round_w1(w1_upper[a], copies, new_rounded(PACK * KP))[:], f"w1_upper{a}")
 
-        feature(banks, 0, 0)
+        for t in range(2):
+            lower_feature(banks[t], t, act.tile([P, S], F32, name="gelu"))
+            banks.append(first_product(lower_q, 2 + t, t))
         w1_q = [upper_w1(0, on_scalar)]
-        feature(banks, 0, 1, staged(3, [P, S], F32))
+        lower_feature(banks[2], 2, staged(3, [P, S], F32))
         w1_q.append(upper_w1(1, on_scalar))
-        feature(banks, 0, 2, staged(4, [P, S], F32))
+        lower_feature(banks[3], 3, staged(4, [P, S], F32))
         w1_q.append(upper_w1(2, shared))
-        feature(banks, 0, 3, staged(1, [P, S], F32))
 
         for a in range(H_PASSES):
             for cols in (lower, upper):
                 nc.scalar.copy(out=deal(w2_codes[:, a, cols]), in_=undealt(w2_raw[:, a, cols]))
 
         w3_raw = []
-        for b, slot in enumerate((3, 2)):
+        for b, slot in enumerate((5, 0)):
             t = staged(slot, [P, PACK, N], F32)
             nc.sync.dma_start(out=t[:], in_=w3[b * KP : (b + 1) * KP, :].rearrange("(p j) n -> p j n", j=PACK))
             w3_raw.append(t)
@@ -224,16 +248,14 @@ def tile_list_udder_health_watch_kernel(
         with nc.allow_non_contiguous_dma(reason="one bias value a partition"):
             nc.sync.dma_start(out=b3_sb[:], in_=b3.rearrange("(c p) -> p c", p=P))
 
-        banks = first_product(w1_q)
-        feature(banks, 1, 0)
-        feature(banks, 1, 1)
-        x_q = [quantise(round_x(0, slice(0, HALF)), "x0_left")]
-        feature(banks, 1, 2)
-        x_q[0] = x_q[0] + quantise(round_x(0, slice(HALF, PAIRS)), "x0_right")
-        feature(banks, 1, 3, piece=QUARTER)
+        banks = [first_product(w1_q, t, (t + 2) % 4) for t in range(PACK)]
+        x_lower = [lower_x(slice(c, c + HALF)) for c in range(0, PAIRS, HALF)]
+        x_q = [quantise(x_lower[0][:], "x0_left") + quantise(x_lower[1][:], "x0_right")]
+        for t in range(PACK):
+            upper_feature(banks[t], t, QUARTER if t == PACK - 1 else HALF)
 
         quarters = [slice(c, c + QUARTER) for c in range(0, PAIRS, QUARTER)]
-        x_q.append([quantise(round_x(1, cols), f"x1_{u}")[0] for u, cols in enumerate(quarters)])
+        x_q.append([quantise(upper_x(cols)[:], f"x1q_{u}")[0] for u, cols in enumerate(quarters)])
         w3_q = []
         for b in range(H_PASSES):
             r = new_rounded(PACK * N)
@@ -276,7 +298,7 @@ def tile_list_udder_health_watch_kernel(
         ys = {}
         for u in range(len(quarters)):
             for b in range(H_PASSES):
-                ys[u, b] = psum.tile([P, PACK, QUARTER], F32, name="bank")
+                ys[u, b] = bank((2 * u + b + 4) % 8, [P, PACK, QUARTER])
                 second_pass(ys[u, b], u, b, 0)
         z_bf = {}
         for u, cols in enumerate(quarters):
@@ -286,7 +308,7 @@ def tile_list_udder_health_watch_kernel(
                 nc.vector.tensor_tensor(
                     woven(z_bf[u, b][:]), by_lines(ys[u, b], slice(0, QUARTER)), by_lines(evening[b], cols), ALU.max
                 )
-            acc = psum.tile([P, N_TILES, QUARTER], F32, name="bank")
+            acc = bank((2 * u + 4) % 8, [P, N_TILES, QUARTER])
             for b in range(H_PASSES):
                 third_pass(acc, u, b)
             store(acc, u)

from contextlib import ExitStack

import concourse.mybir as mybir

T, S, PAIRS, K, H, N = 2048, 1024, 512, 1536, 1024, 384
FLOPS = 2 * (K * H * S + H * H * PAIRS + H * N * PAIRS)

F32 = mybir.dt.float32
BF16 = mybir.dt.bfloat16
I32 = mybir.dt.int32
U32 = mybir.dt.uint32
U16 = mybir.dt.uint16
U8 = mybir.dt.uint8
FP8X4 = mybir.dt.float8_e4m3fn_x4
FP4X4 = mybir.dt.float4_e2m1fn_x4
ALU = mybir.AluOpType
ACT = mybir.ActivationFunctionType

P = 128
PACK = 4
KP = P * PACK
BANK = 512
K_PASSES = K // KP
H_PASSES = H // KP
N_TILES = N // P
QUARTER = 128
HALF = 256
PLANE_ROW = (0, 8, 4)


def tile_list_udder_health_watch_kernel(
    tc, tab_words, tab_scales, w1, b1, gain, w2_words, w2_scales, w3, b3, offs, pos1, pos2, out
):
    nc = tc.nc
    with ExitStack() as ctx:
        keep = ctx.enter_context(tc.tile_pool(name="keep", bufs=1))
        stage = ctx.enter_context(tc.tile_pool(name="stage", bufs=1))
        rounded = ctx.enter_context(tc.tile_pool(name="rounded", bufs=3))
        feat = ctx.enter_context(tc.tile_pool(name="feat", bufs=4))
        act = ctx.enter_context(tc.tile_pool(name="act", bufs=2))
        psum = ctx.enter_context(tc.psum_pool(name="psum", bufs=1))

        offs_sb = keep.tile([P, S // 16], U16, name="offs_sb")
        pos1_sb = keep.tile([P, PAIRS // 16], U16, name="pos1_sb")
        pos2_sb = keep.tile([P, PAIRS // 16], U16, name="pos2_sb")
        picked = [keep.tile([P, S], U32, name=f"picked{a}", align_bytes=64) for a in range(K_PASSES)]
        picked_rows = keep.tile([P, S], U8, name="picked_rows", align_bytes=64)
        picked_plane = keep.tile([P, S], U8, name="picked_plane", align_bytes=64)
        b1_sb = keep.tile([P, H_PASSES, PACK], F32, name="b1_sb")
        gain_sb = keep.tile([P, H_PASSES, PACK], F32, name="gain_sb")
        w2_codes = keep.tile([P, H_PASSES, H], U16, name="w2_codes", align_bytes=64)
        evening = [keep.tile([P, PACK, PAIRS], F32, name=f"evening{b}") for b in range(H_PASSES)]
        morning = keep.tile([P, PACK, PAIRS], F32, name="morning")
        minus_x = keep.tile([P, PACK, PAIRS], F32, name="minus_x")
        gains = keep.tile([P, PACK, PAIRS], F32, name="gains")

        def staged(slot, shape, dtype):
            return stage.tile(shape, dtype, name=f"stage{slot}")

        def load_words(a, slot):
            t = staged(slot, [P, T], I32)
            nc.sync.dma_start(out=t[:], in_=tab_words[a].rearrange("p t i -> p (t i)").bitcast(I32))
            return t

        def w1_rows(a, cols):
            return w1[a * KP : (a + 1) * KP, cols].rearrange("(p j) c -> p j c", j=PACK)

        def load_w1(a, cols, slot):
            t = staged(slot, [P, PACK, KP], F32)
            nc.sync.dma_start(out=t[:], in_=w1_rows(a, cols))
            return [t[:, :, :HALF], t[:, :, HALF:]]

        def load_w1_halves(a, slot):
            t = staged(slot, [P, 2, PACK, HALF], F32)
            for i in range(2):
                nc.sync.dma_start(out=t[:, i], in_=w1_rows(a, slice(i * HALF, (i + 1) * HALF)))
            return [t[:, 0], t[:, 1]]

        def quantise(src, name, after=None):
            words = src.shape[1] // PACK
            codes = keep.tile([P, words], U32, name=after or name + "_codes", align_bytes=64)
            plane = keep.tile([P, words], U8, name=name + "_plane", align_bytes=64)
            nc.vector.quantize_mx(out=codes[:].bitcast(FP8X4), scales=plane[:], in_=src)
            return [(codes[:, c : c + P], plane[:, c : c + P]) for c in range(0, words, P)]

        def round_w1(parts, copies, r):
            for i, copy in enumerate(copies):
                copy(
                    out=r[:].rearrange("p (t q j) -> p q j t", t=PACK, j=PACK)[:, i * P // 2 : (i + 1) * P // 2],
                    in_=parts[i].rearrange("p j (q t) -> p q j t", t=PACK),
                )
            return r

        def new_rounded(width):
            return rounded.tile([P, width], BF16, name="rounded", align_bytes=64)

        def bank(i, shape):
            return psum.tile(shape, F32, name=f"bank{i}")

        def first_product(w1_q, t, where):
            if True:
                pair = [bank(2 * where + half, [P, BANK]) for half in range(S // BANK)]
                for a in range(K_PASSES):
                    codes, plane = w1_q[a][t]
                    for half in range(S // BANK):
                        cols = slice(half * BANK, (half + 1) * BANK)
                        nc.tensor.matmul_mx(
                            out=pair[half][:],
                            lhsT=codes.bitcast(FP8X4),
                            lhsT_scale=plane,
                            rhs=picked[a][:, cols].bitcast(FP8X4),
                            rhs_scale=picked_plane[PLANE_ROW[a] : P, cols],
                            start=(a == 0),
                            stop=(a == K_PASSES - 1),
                        )
            return pair

        def gelu(banks, b, t, g):
            for half in range(S // BANK):
                nc.scalar.activation(
                    out=g[:, half * BANK : (half + 1) * BANK],
                    in_=banks[half][:],
                    func=ACT.Gelu_apprx_tanh,
                    bias=b1_sb[:, b, t : t + 1],
                )

        def lower_feature(banks, t, g):
            gelu(banks, 0, t, g)
            nc.vector.tensor_tensor(evening[0][:, t, :], g[:].indirect(pos1_sb[:]), gains[:, t, :], ALU.mult)
            nc.vector.tensor_tensor(morning[:, t, :], g[:].indirect(pos2_sb[:]), gains[:, t, :], ALU.mult)

        def upper_feature(banks, t, piece):
            g = act.tile([P, S], F32, name="gelu")
            gelu(banks, 1, t, g)
            h = feat.tile([P, S], F32, name="feat")
            for c in range(0, S, BANK):
                nc.scalar.activation(
                    out=h[:, c : c + BANK], in_=g[:, c : c + BANK], func=ACT.Copy, scale=gain_sb[:, 1, t : t + 1]
                )
            for c in range(0, PAIRS, piece):
                cols, entries = slice(c, c + piece), slice(c // 16, (c + piece) // 16)
                nc.vector.tensor_copy(out=evening[1][:, t, cols], in_=h[:].indirect(pos1_sb[:, entries]))
                nc.vector.tensor_tensor(
                    minus_x[:, t, cols], h[:].indirect(pos2_sb[:, entries]), evening[1][:, t, cols], ALU.subtract
                )

        def by_lines(tile3, cols):
            return tile3[:, :, cols].rearrange("p t (c i) -> p c t i", i=PACK)

        def woven(flat):
            return flat.rearrange("p (c i t) -> p c t i", i=PACK, t=PACK)

        def lower_x(cols):
            flat = keep.tile([P, PACK * HALF], BF16, name=f"x0_{cols.start}", align_bytes=64)
            nc.vector.tensor_tensor(woven(flat[:]), by_lines(evening[0], cols), by_lines(morning, cols), ALU.subtract)
            return flat

        def upper_x(cols):
            flat = keep.tile([P, PACK * QUARTER], BF16, name=f"x1_{cols.start}", align_bytes=64)
            nc.scalar.activation(out=woven(flat[:]), in_=by_lines(minus_x, cols), func=ACT.Copy, scale=-1.0)
            return flat

        def deal(tile2):
            return tile2.rearrange("p (g t q) -> p g q t", t=PACK, q=P)

        def undealt(tile2):
            return tile2.rearrange("p (g q t) -> p g q t", t=PACK, q=P)

        on_scalar = (nc.scalar.copy, nc.scalar.copy)
        shared = (nc.scalar.copy, nc.vector.tensor_copy)
        lower, upper = slice(0, KP), slice(KP, H)

        nc.vector.memset(picked_plane[:].bitcast(I32), 0)
        nc.sync.dma_start(offs_sb[:], offs)
        tab_sb = [load_words(0, 2)]
        tab_rows = staged(1, [P, T // 4], I32)
        nc.gpsimd.memset(tab_rows[:], 0)
        for s in range(2):
            nc.sync.dma_start(
                out=tab_rows[s:P:8, :], in_=tab_scales[0:2, s:16:2, :].rearrange("a g c -> g a c").bitcast(I32)
            )
            nc.sync.dma_start(out=tab_rows[4 + s : P : 16, :], in_=tab_scales[2, s:16:2, :].bitcast(I32))
        nc.sync.dma_start(out=gain_sb[:], in_=gain.rearrange("(b p t) -> p b t", b=H_PASSES, t=PACK))
        w1_lower0 = load_w1(0, lower, 0)
        nc.sync.dma_start(out=b1_sb[:], in_=b1.rearrange("(b p t) -> p b t", b=H_PASSES, t=PACK))
        nc.sync.dma_start(pos1_sb[:], pos1)
        nc.sync.dma_start(pos2_sb[:], pos2)
        tab_sb.extend(load_words(a, 2 + a) for a in range(1, K_PASSES))
        w1_lower1 = load_w1_halves(1, 5)

        nc.vector.tensor_copy(out=picked_rows[:], in_=tab_rows[:].bitcast(U8).indirect(offs_sb[:]))
        for s in range(2):
            nc.sync.dma_start(out=picked_plane[s:P:4, :].bitcast(I32), in_=picked_rows[s:P:4, :].bitcast(I32))
            nc.sync.dma_start(
                out=picked_plane[2 + s : P - 16 : 4, :].bitcast(I32), in_=picked_rows[16 + s : P : 4, :].bitcast(I32)
            )
        w1_lower2 = load_w1_halves(2, 1)
        w2_raw_plane = staged(0, [P, H_PASSES * H], U8)
        nc.gpsimd.memset(w2_raw_plane[:].bitcast(I32), 0)
        for r in range(4):
            nc.sync.dma_start(
                out=w2_raw_plane[r:P:32, :].rearrange("q (a c) -> q a c", a=H_PASSES).bitcast(I32),
                in_=w2_scales[:, r:16:4, :].rearrange("a q c -> q a c").bitcast(I32),
            )

        w1_q = [quantise(round_w1(w1_lower0, on_scalar, new_rounded(PACK * KP))[:], "w1_lower0")]
        nc.scalar.copy(out=gains[:], in_=gain_sb[:, 0, :].unsqueeze(2).to_broadcast([P, PACK, PAIRS]))
        for a in range(K_PASSES):
            nc.vector.tensor_copy(out=picked[a][:], in_=tab_sb[a][:].bitcast(U32).indirect(offs_sb[:]))
        r1 = round_w1(w1_lower1, shared, new_rounded(PACK * KP))
        first1 = quantise(r1[:, :KP], "w1_first1")
        r2 = keep.tile([P, PACK * KP], BF16, name="last", align_bytes=64)
        round_w1(w1_lower2, shared, r2)
        first2 = quantise(r2[:, :KP], "w1_first2")
        w1_q.append(first1 + quantise(r1[:, KP:], "w1_rest1"))
        w1_q.append(first2 + quantise(r2[:, KP:], "w1_rest2"))
        lower_q = w1_q
        banks = [first_product(lower_q, t, t) for t in range(2)]
        w2_plane = keep.tile([P, H_PASSES * H], U8, name="last", align_bytes=64)
        nc.vector.tensor_copy(out=deal(w2_plane[:]), in_=undealt(w2_raw_plane[:]))

        w1_upper = [load_w1(a, upper, slot) for a, slot in enumerate((3, 4, 5))]
        w2_raw = staged(1, [P, H_PASSES, H], U16)
        nc.sync.dma_start(out=w2_raw[:].bitcast(I32), in_=w2_words.rearrange("a p c -> p a c").bitcast(I32))

        def upper_w1(a, copies):
            return quantise(round_w1(w1_upper[a], copies, new_rounded(PACK * KP))[:], f"w1_upper{a}")

        for t in range(2):
            lower_feature(banks[t], t, act.tile([P, S], F32, name="gelu"))
            banks.append(first_product(lower_q, 2 + t, t))
        w1_q = [upper_w1(0, on_scalar)]
        lower_feature(banks[2], 2, staged(3, [P, S], F32))
        w1_q.append(upper_w1(1, on_scalar))
        lower_feature(banks[3], 3, staged(4, [P, S], F32))
        w1_q.append(upper_w1(2, shared))

        for a in range(H_PASSES):
            for cols in (lower, upper):
                nc.scalar.copy(out=deal(w2_codes[:, a, cols]), in_=undealt(w2_raw[:, a, cols]))

        w3_raw = []
        for b, slot in enumerate((5, 0)):
            t = staged(slot, [P, PACK, N], F32)
            nc.sync.dma_start(out=t[:], in_=w3[b * KP : (b + 1) * KP, :].rearrange("(p j) n -> p j n", j=PACK))
            w3_raw.append(t)
        b3_sb = staged(4, [P, N_TILES], F32)
        with nc.allow_non_contiguous_dma(reason="one bias value a partition"):
            nc.sync.dma_start(out=b3_sb[:], in_=b3.rearrange("(c p) -> p c", p=P))

        banks = [first_product(w1_q, t, (t + 2) % 4) for t in range(PACK)]
        x_lower = [lower_x(slice(c, c + HALF)) for c in range(0, PAIRS, HALF)]
        x_q = [quantise(x_lower[0][:], "x0_left") + quantise(x_lower[1][:], "x0_right")]
        for t in range(PACK):
            upper_feature(banks[t], t, QUARTER if t == PACK - 1 else HALF)

        quarters = [slice(c, c + QUARTER) for c in range(0, PAIRS, QUARTER)]
        x_q.append([quantise(upper_x(cols)[:], f"x1q_{u}")[0] for u, cols in enumerate(quarters)])
        w3_q = []
        for b in range(H_PASSES):
            r = new_rounded(PACK * N)
            nc.scalar.copy(out=woven(r[:]), in_=by_lines(w3_raw[b], slice(0, N)))
            w3_q.append(quantise(r[:], f"w3_{b}", after=f"x1_{quarters[b].start}"))

        def second_pass(y, u, b, a):
            x_codes, x_plane = x_q[a][u]
            for t in range(PACK):
                m = b * KP + t * P
                nc.tensor.matmul_mx(
                    out=y[:, t, :],
                    lhsT=w2_codes[:, a, m : m + P].bitcast(FP4X4),
                    lhsT_scale=w2_plane[:, a * H + m : a * H + m + P],
                    rhs=x_codes.bitcast(FP8X4),
                    rhs_scale=x_plane,
                    start=(a == 0 and t == 0),
                    stop=(a == H_PASSES - 1 and t == PACK - 1),
                )

        def third_pass(acc, u, b):
            z_codes, z_plane = quantise(z_bf[u, b][:], f"z{u}{b}")[0]
            for c in range(N_TILES):
                nc.tensor.matmul_mx(
                    out=acc[:, c, :],
                    lhsT=w3_q[b][c][0].bitcast(FP8X4),
                    lhsT_scale=w3_q[b][c][1],
                    rhs=z_codes.bitcast(FP8X4),
                    rhs_scale=z_plane,
                    start=(b == 0 and c == 0),
                    stop=(b == H_PASSES - 1 and c == N_TILES - 1),
                )

        def store(acc, u):
            res = keep.tile([P, N_TILES, QUARTER], F32, name=f"res{u}")
            for c in range(N_TILES):
                nc.scalar.activation(out=res[:, c, :], in_=acc[:, c, :], func=ACT.Identity, bias=b3_sb[:, c : c + 1])
            nc.sync.dma_start(out=out[:, quarters[u]].rearrange("(c p) j -> p c j", p=P), in_=res[:])

        ys = {}
        for u in range(len(quarters)):
            for b in range(H_PASSES):
                ys[u, b] = bank((2 * u + b + 4) % 8, [P, PACK, QUARTER])
                second_pass(ys[u, b], u, b, 0)
        z_bf = {}
        for u, cols in enumerate(quarters):
            for b in range(H_PASSES):
                second_pass(ys[u, b], u, b, 1)
                z_bf[u, b] = keep.tile([P, KP], BF16, name=f"z_bf{u}{b}", align_bytes=64)
                nc.vector.tensor_tensor(
                    woven(z_bf[u, b][:]), by_lines(ys[u, b], slice(0, QUARTER)), by_lines(evening[b], cols), ALU.max
                )
            acc = bank((2 * u + 4) % 8, [P, N_TILES, QUARTER])
            for b in range(H_PASSES):
                third_pass(acc, u, b)
            store(acc, u)
